import numpy as np
import ml_dtypes


def mxq(x, axis, fmt="e4m3"):
    dtype, down = {"e4m3": (ml_dtypes.float8_e4m3fn, 7), "e5m2": (ml_dtypes.float8_e5m2, 14)}[fmt]
    v = np.moveaxis(np.asarray(x, np.float32).astype(ml_dtypes.bfloat16).astype(np.float64), axis, -1)
    blocks = v.reshape(v.shape[:-1] + (-1, 32))
    amax = np.abs(blocks).max(-1, keepdims=True)
    byte = np.maximum(np.where(amax > 0, np.frexp(amax)[1] - 1 + 127, 0) - down, 1)
    scale = np.exp2(byte - 127.0)
    codes = (blocks / scale).astype(np.float32).astype(dtype).astype(np.float64)
    return np.moveaxis((codes * scale).reshape(v.shape), -1, axis)


WIDE = False


def mx_kscale(k):
    if not WIDE:
        return np.ones(k)
    levels = np.array([10, -10, 5, -5, 0])
    if k % 512:
        return np.exp2(np.random.permutation(np.resize(levels, k // 32))).repeat(32)
    a = np.empty((k // 512, 16))
    for p in range(k // 512):
        a[p, :8] = np.random.permutation(np.resize(levels, 8))
        for g in range(8):
            far = levels[np.abs(levels - a[p, g]) >= 10]
            a[p, g + 8] = far[np.random.randint(len(far))]
    return np.exp2(a.ravel()).repeat(32)


def f64(x):
    return np.asarray(x).astype(np.float64)


def striped(idx):
    return np.tile(np.asarray(idx).reshape(-1, 16).T, (8, 1)).astype(np.uint16)


def unstriped(offs):
    return offs[:16].T.reshape(-1).astype(np.int64)


E2M1 = np.array([0.0, 0.5, 1.0, 1.5, 2.0, 3.0, 4.0, 6.0, -0.0, -0.5, -1.0, -1.5, -2.0, -3.0, -4.0, -6.0])


def pack_weight(w, fmt):
    k, n = w.shape
    w = f64(np.asarray(w, np.float32).astype(ml_dtypes.bfloat16)).reshape(k // 32, 32, n)
    amax = np.abs(w).max(1)
    if fmt == "e4m3":
        byte = np.frexp(amax)[1] - 1 + 127 - 7
    else:
        mant, ex = np.frexp(amax / 6.0)
        byte = np.where(mant > 0.5, ex, ex - 1) + 127
    byte = np.clip(np.where(amax > 0, byte, 1), 1, 254)
    scaled = (w * np.exp2(127.0 - byte)[:, None, :]).reshape(k, n).astype(np.float32)
    by_word = np.ascontiguousarray(scaled.reshape(k // 512, 128, 4, n).transpose(0, 1, 3, 2))
    if fmt == "e4m3":
        words = by_word.astype(ml_dtypes.float8_e4m3fn).view(np.uint8)
    else:
        c = by_word.astype(ml_dtypes.float4_e2m1fn).view(np.uint8) & 0xF
        words = (c[..., 0::2] | (c[..., 1::2] << 4)).reshape(k // 512, 128, 2 * n)
    return np.ascontiguousarray(words), np.ascontiguousarray(byte.astype(np.uint8).reshape(k // 512, 16, n))


def unpack_weight(words, scales, fmt):
    g, _, n = scales.shape
    words = np.ascontiguousarray(words).reshape(g, 128, n, -1)
    if fmt == "e4m3":
        vals = words.view(ml_dtypes.float8_e4m3fn).astype(np.float64)
    else:
        nib = np.empty((g, 128, n, 4), np.uint8)
        nib[..., 0::2] = words & 0xF
        nib[..., 1::2] = words >> 4
        vals = E2M1[nib]
    vals = vals * np.repeat(np.exp2(scales.astype(np.float64) - 127.0), 8, axis=1)[..., None]
    return vals.transpose(0, 1, 3, 2).reshape(g * 512, n)


def bf(x):
    return np.asarray(x, np.float32).astype(ml_dtypes.bfloat16)


def planes(Y):
    r, m = Y.shape
    b = f64(bf(Y)).reshape(r // 32, 32, m)
    amax = np.abs(b).max(1)
    byte = np.clip(np.where(amax > 0, np.frexp(amax)[1] - 1 + 127 - 7, 1), 1, 254)
    codes = (b * np.exp2(127.0 - byte)[:, None, :]).reshape(r, m).astype(np.float32).astype(ml_dtypes.float8_e4m3fn).view(np.uint8)
    words = codes.reshape(r // 512, 128, 4, m).transpose(0, 1, 3, 2)
    return np.ascontiguousarray(words), np.ascontiguousarray(byte.astype(np.uint8).reshape(r // 512, 16, m))


D, T, I, Q, E, U, M = 512, 2048, 512, 256, 512, 1024, 1024


def setup_inputs():
    n = np.random.standard_normal
    idx = np.random.permutation(T)[:I]
    idx2 = np.random.permutation(U)[:I]
    idx3 = np.random.permutation(M)[:Q]
    fd = mx_kscale(D)
    fi = mx_kscale(I)
    ti = np.ones(T)
    ti[idx] = fi
    keysp = pack_weight(n((D, T)) / fd[:, None], "e2m1")
    return {
        "query": (n((D, Q)) * 0.7 / np.sqrt(D) * fd[:, None]).astype(np.float32),
        "query2": (n((D, Q)) * 0.7 / np.sqrt(D) * fd[:, None]).astype(np.float32),
        "keys_words": keysp[0],
        "keys_scales": keysp[1],
        "notes": (n((D, U)) / fd[:, None]).astype(np.float32),
        "os": (np.random.uniform(0.02, 0.08, (1, I)) * fi).astype(np.float32),
        "vals": (n((E, T)) / ti).astype(np.float32),
        "member": (n((E, M))).astype(np.float32),
        "offs": striped(idx),
        "offs2": striped(idx2),
        "offs3": striped(idx3),
    }


def reference(query, query2, keys_words, keys_scales, notes, os, vals, member, offs, offs2, offs3):
    idx = unstriped(offs)
    idx2 = unstriped(offs2)
    idx3 = unstriped(offs3)
    keysu = unpack_weight(keys_words, keys_scales, "e2m1")
    queryq = mxq(f64(query), 0, "e4m3")
    keysidxg = keysu[:, idx]
    query2q = mxq(f64(query2), 0, "e4m3")
    notesidx2q = mxq(f64(notes)[:, idx2], 0, "e4m3")
    s = queryq.T @ keysidxg + query2q.T @ notesidx2q
    w = np.maximum(s, 0.0)
    wo1 = w * f64(os)
    wt1 = wo1.T
    vt1 = f64(vals)[:, idx].T
    vt1q = mxq(vt1, 0, "e4m3")
    wt1q = mxq(wt1, 0, "e4m3")
    o = vt1q.T @ wt1q
    y = np.abs(o - f64(member)[:, idx3])
    words, scales = planes(y)
    return y, words, scales

@@ -1,0 +1,226 @@
+from contextlib import ExitStack
+
+import concourse.mybir as mybir
+from concourse.masks import make_identity
+
+D, T, I, Q, E, U, M = 512, 2048, 512, 256, 512, 1024, 1024
+FLOPS = 2 * Q * I * D * 2 + 2 * E * Q * I
+
+F32 = mybir.dt.float32
+BF16 = mybir.dt.bfloat16
+I32 = mybir.dt.int32
+U32 = mybir.dt.uint32
+U16 = mybir.dt.uint16
+U8 = mybir.dt.uint8
+FP8X4 = mybir.dt.float8_e4m3fn_x4
+FP4X4 = mybir.dt.float4_e2m1fn_x4
+ALU = mybir.AluOpType
+ACT = mybir.ActivationFunctionType
+
+P = 128
+PACK = 4
+
+
+def tile_attend_twosources_distanceout_lean_pl_kernel(
+    tc, query, query2, keys_words, keys_scales, notes, slot_factor, vals, member, offs, offs2, offs3, out_0, out_1, out_2
+):
+    nc = tc.nc
+    with ExitStack() as ctx:
+        sb = ctx.enter_context(tc.tile_pool(name="sb", bufs=1))
+        ps = ctx.enter_context(tc.psum_pool(name="ps", bufs=1))
+        ps_turn = ctx.enter_context(tc.psum_pool(name="ps_turn", bufs=2))
+
+        def tile(shape, dtype, name, tag=None):
+            return sb.tile(shape, dtype, name=name, tag=tag or name, align_bytes=64)
+
+        def planes_of(dram):
+            return dram.rearrange("(p r) c -> p r c", r=PACK)
+
+        token_list = tile([P, I // 16], U16, "token_list")
+        note_list = tile([P, I // 16], U16, "note_list")
+        member_list = tile([P, Q // 16], U16, "member_list")
+        key_words = tile([P, T], U16, "key_words")
+        key_scales = tile([P, T], U8, "key_scales")
+        factor = tile([P, PACK], F32, "factor")
+        note_planes = [tile([P, U], F32, f"notes{r}") for r in range(PACK)]
+        val_planes = [tile([P, T], F32, f"vals{r}") for r in range(PACK)]
+        member_planes = [tile([P, M], F32, f"member{r}") for r in range(PACK)]
+        query_rows = [tile([P, PACK, Q], F32, f"query{j}") for j in range(2)]
+
+        nc.vector.memset(key_scales[:].bitcast(I32), 0)
+        for quad in range(4):
+            nc.scalar.dma_start(
+                key_scales[32 * quad : 32 * quad + 4, :].bitcast(I32),
+                keys_scales[0, 4 * quad : 4 * quad + 4, :].bitcast(I32),
+            )
+        nc.scalar.dma_start(factor[:], slot_factor.rearrange("o (p t) -> (o p) t", t=PACK))
+        nc.sync.dma_start(key_words[:].bitcast(I32), keys_words[0].bitcast(I32))
+        nc.sync.dma_start(token_list[:], offs)
+        nc.sync.dma_start(note_planes[0][:], planes_of(notes)[:, 0, :])
+        nc.sync.dma_start(note_list[:], offs2)
+        for r in range(1, PACK):
+            nc.sync.dma_start(note_planes[r][:], planes_of(notes)[:, r, :])
+        nc.sync.dma_start(query_rows[0][:], planes_of(query))
+        nc.sync.dma_start(query_rows[1][:], planes_of(query2))
+        nc.sync.dma_start(member_list[:], offs3)
+        for r in range(PACK):
+            nc.sync.dma_start(val_planes[r][:], planes_of(vals)[:, r, :])
+        for r in range(PACK):
+            nc.sync.dma_start(member_planes[r][:], planes_of(member)[:, r, :])
+
+        identity = tile([P, P], F32, "identity")
+        make_identity(nc, identity[:])
+
+        listed_words = tile([P, I], U16, "listed_words")
+        nc.vector.tensor_copy(listed_words[:], key_words[:].indirect(token_list[:]))
+        key_codes = tile([P, I], U16, "key_codes")
+        nc.vector.tensor_copy(
+            key_codes[:].rearrange("p (t s) -> p s t", t=PACK), listed_words[:].rearrange("p (s t) -> p s t", t=PACK)
+        )
+        key_code_scales = tile([P, I], U8, "key_code_scales")
+        nc.vector.tensor_copy(
+            key_code_scales[:].rearrange("p (t s) -> p s t", t=PACK), key_scales[:].indirect(token_list[:])
+        )
+
+        listed_notes = tile([P, PACK, I], BF16, "listed_notes")
+        for r in range(PACK):
+            window = note_planes[r][:].indirect(note_list[:])
+            if r % 2 == 0:
+                nc.scalar.activation(listed_notes[:, r, :], window, ACT.Copy)
+            else:
+                nc.vector.tensor_copy(listed_notes[:, r, :], window)
+        notes_woven = tile([P, I * PACK], BF16, "notes_woven")
+        nc.vector.tensor_copy(
+            notes_woven[:].rearrange("p (t s r) -> p s r t", t=PACK, r=PACK),
+            listed_notes[:].rearrange("p r (s t) -> p s r t", t=PACK),
+        )
+        note_codes = tile([P, I], U32, "note_codes")
+        note_scales = tile([P, I], U8, "note_scales")
+        nc.vector.quantize_mx(note_codes[:].bitcast(FP8X4), note_scales[:], notes_woven[:])
+
+        query_codes, query_scales = [], []
+        for j in range(2):
+            woven = tile([P, Q * PACK], BF16, f"query_woven{j}")
+            nc.scalar.copy(
+                woven[:].rearrange("p (c i r) -> p c r i", i=4, r=PACK),
+                query_rows[j][:].rearrange("p r (c i) -> p c r i", i=4),
+            )
+            codes = tile([P, Q], U32, f"query_codes{j}")
+            scales = tile([P, Q], U8, f"query_scales{j}")
+            nc.vector.quantize_mx(codes[:].bitcast(FP8X4), scales[:], woven[:])
+            query_codes.append(codes)
+            query_scales.append(scales)
+
+        weights_woven = tile([P, Q * PACK], BF16, "weights_woven")
+        for h in range(Q // P):
+            q_cols = slice(h * P, (h + 1) * P)
+            scores = ps.tile([P, PACK, P], F32, name=f"scores{h}")
+            for t in range(PACK):
+                slots = slice(t * P, (t + 1) * P)
+                nc.tensor.matmul_mx(
+                    scores[:, t, :],
+                    lhsT=key_codes[:, slots].bitcast(FP4X4),
+                    lhsT_scale=key_code_scales[:, slots],
+                    rhs=query_codes[0][:, q_cols].bitcast(FP8X4),
+                    rhs_scale=query_scales[0][:, q_cols],
+                    start=True,
+                    stop=False,
+                )
+                nc.tensor.matmul_mx(
+                    scores[:, t, :],
+                    lhsT=note_codes[:, slots].bitcast(FP8X4),
+                    lhsT_scale=note_scales[:, slots],
+                    rhs=query_codes[1][:, q_cols].bitcast(FP8X4),
+                    rhs_scale=query_scales[1][:, q_cols],
+                    start=False,
+                    stop=True,
+                )
+            nc.vector.scalar_tensor_tensor(
+                weights_woven[:, h * P * PACK : (h + 1) * P * PACK].rearrange("p (q t) -> p q t", t=PACK),
+                scores[:].rearrange("p t q -> p q t"),
+                0.0,
+                factor[:].unsqueeze(1).to_broadcast([P, P, PACK]),
+                ALU.max,
+                ALU.mult,
+            )
+        weight_codes = tile([P, Q], U32, "weight_codes")
+        weight_scales = tile([P, Q], U8, "weight_scales")
+        nc.vector.quantize_mx(weight_codes[:].bitcast(FP8X4), weight_scales[:], weights_woven[:])
+
+        sums = []
+        dist = tile([P, PACK, Q], F32, "dist")
+        halves = [slice(0, Q // 2), slice(Q // 2, Q)]
+
+        def gather_values(r):
+            listed_vals = tile([P, I], BF16, f"listed_vals{r}")
+            if r < PACK - 1:
+                nc.scalar.activation(listed_vals[:], val_planes[r][:].indirect(token_list[:]), ACT.Copy)
+            else:
+                nc.vector.tensor_copy(listed_vals[:, : I // 2], val_planes[r][:].indirect(token_list[:, : I // 32]))
+                nc.scalar.activation(
+                    listed_vals[:, I // 2 :], val_planes[r][:].indirect(token_list[:, I // 32 :]), ACT.Copy
+                )
+            return listed_vals
+
+        def multiply(r, listed_vals):
+            pairs = listed_vals[:].bitcast(F32)
+            turned = ps_turn.tile([P, 2, P], F32, name="turned")
+            for u in range(2):
+                nc.tensor.transpose(turned[:, u, :], pairs[:, u::2], identity[:])
+            vals_woven = tile([P, P * PACK], BF16, f"vals_woven{r}", tag="vals3" if r == PACK - 2 else None)
+            copy_out = nc.vector.tensor_copy if r < PACK - 1 else nc.scalar.copy
+            copy_out(
+                vals_woven[:].bitcast(F32).rearrange("p (c u) -> p c u", u=2), turned[:].rearrange("p u c -> p c u")
+            )
+            val_codes = tile([P, P], U32, f"val_codes{r}")
+            val_scales = tile([P, P], U8, f"val_scales{r}")
+            nc.vector.quantize_mx(val_codes[:].bitcast(FP8X4), val_scales[:], vals_woven[:])
+            acc = ps.tile([P, Q], F32, name=f"acc{r}")
+            nc.tensor.matmul_mx(
+                acc[:],
+                lhsT=val_codes[:].bitcast(FP8X4),
+                lhsT_scale=val_scales[:],
+                rhs=weight_codes[:].bitcast(FP8X4),
+                rhs_scale=weight_scales[:],
+                start=True,
+                stop=True,
+            )
+            o_plane = tile([P, Q], F32, f"o{r}")
+            copy_out = nc.vector.tensor_copy if r < PACK - 2 else nc.scalar.copy
+            copy_out(o_plane[:], acc[:])
+            sums.append(o_plane)
+
+        def distance(r):
+            diff = tile([P, Q], F32, f"diff{r}")
+            for cols in halves if r == PACK - 1 else [slice(0, Q)]:
+                listed = member_planes[r][:].indirect(member_list[:, cols.start // 16 : cols.stop // 16])
+                nc.vector.tensor_tensor(diff[:, cols], listed, sums[r][:, cols], ALU.subtract)
+                nc.scalar.activation(dist[:, r, cols], diff[:, cols], ACT.Abs)
+            nc.sync.dma_start(planes_of(out_0)[:, r, :], dist[:, r, :])
+
+        listed = [gather_values(r) for r in range(PACK)]
+        for r in range(PACK):
+            multiply(r, listed[r])
+        for r in range(PACK):
+            distance(r)
+        dist_woven = tile([P, Q * PACK], BF16, "dist_woven")
+        dist_codes = tile([P, Q], U32, "dist_codes")
+        dist_scales = tile([P, Q], U8, "dist_scales")
+        for cols in halves:
+            nc.vector.tensor_copy(
+                dist_woven[:, cols.start * PACK : cols.stop * PACK].rearrange("p (c i r) -> p c r i", i=4, r=PACK),
+                dist[:, :, cols].rearrange("p r (c i) -> p c r i", i=4),
+            )
+        for cols in halves:
+            nc.vector.quantize_mx(
+                dist_codes[:, cols].bitcast(FP8X4),
+                dist_scales[:, cols],
+                dist_woven[:, cols.start * PACK : cols.stop * PACK],
+            )
+        nc.sync.dma_start(out_1[0].rearrange("p c r -> p (c r)").bitcast(I32), dist_codes[:].bitcast(I32))
+        for quad in range(4):
+            queue = nc.sync if quad % 2 == 0 else nc.scalar
+            queue.dma_start(
+                out_2[0, 4 * quad : 4 * quad + 4, :].bitcast(I32),
+                dist_scales[32 * quad : 32 * quad + 4, :].bitcast(I32),
+            )

@@ -19,6 +19,7 @@ ACT = mybir.ActivationFunctionType
 
 P = 128
 PACK = 4
+SPLIT = 288
 
 
 def tile_attend_twosources_distanceout_lean_pl_kernel(
@@ -28,7 +29,6 @@ def tile_attend_twosources_distanceout_lean_pl_kernel(
     with ExitStack() as ctx:
         sb = ctx.enter_context(tc.tile_pool(name="sb", bufs=1))
         ps = ctx.enter_context(tc.psum_pool(name="ps", bufs=1))
-        ps_turn = ctx.enter_context(tc.psum_pool(name="ps_turn", bufs=2))
 
         def tile(shape, dtype, name, tag=None):
             return sb.tile(shape, dtype, name=name, tag=tag or name, align_bytes=64)
@@ -49,21 +49,22 @@ def tile_attend_twosources_distanceout_lean_pl_kernel(
 
         nc.vector.memset(key_scales[:].bitcast(I32), 0)
         for quad in range(4):
-            nc.scalar.dma_start(
+            nc.sync.dma_start(
                 key_scales[32 * quad : 32 * quad + 4, :].bitcast(I32),
                 keys_scales[0, 4 * quad : 4 * quad + 4, :].bitcast(I32),
             )
-        nc.scalar.dma_start(factor[:], slot_factor.rearrange("o (p t) -> (o p) t", t=PACK))
-        nc.sync.dma_start(key_words[:].bitcast(I32), keys_words[0].bitcast(I32))
-        nc.sync.dma_start(token_list[:], offs)
         nc.sync.dma_start(note_planes[0][:], planes_of(notes)[:, 0, :])
         nc.sync.dma_start(note_list[:], offs2)
+        nc.sync.dma_start(key_words[:].bitcast(I32), keys_words[0].bitcast(I32))
+        nc.sync.dma_start(token_list[:], offs)
+        nc.sync.dma_start(query_rows[0][:], planes_of(query))
         for r in range(1, PACK):
             nc.sync.dma_start(note_planes[r][:], planes_of(notes)[:, r, :])
-        nc.sync.dma_start(query_rows[0][:], planes_of(query))
         nc.sync.dma_start(query_rows[1][:], planes_of(query2))
+        nc.sync.dma_start(factor[:], slot_factor.rearrange("o (p t) -> (o p) t", t=PACK))
+        nc.sync.dma_start(val_planes[0][:], planes_of(vals)[:, 0, :])
         nc.sync.dma_start(member_list[:], offs3)
-        for r in range(PACK):
+        for r in range(1, PACK):
             nc.sync.dma_start(val_planes[r][:], planes_of(vals)[:, r, :])
         for r in range(PACK):
             nc.sync.dma_start(member_planes[r][:], planes_of(member)[:, r, :])
@@ -85,7 +86,7 @@ def tile_attend_twosources_distanceout_lean_pl_kernel(
         listed_notes = tile([P, PACK, I], BF16, "listed_notes")
         for r in range(PACK):
             window = note_planes[r][:].indirect(note_list[:])
-            if r % 2 == 0:
+            if r < PACK - 1:
                 nc.scalar.activation(listed_notes[:, r, :], window, ACT.Copy)
             else:
                 nc.vector.tensor_copy(listed_notes[:, r, :], window)
@@ -98,7 +99,7 @@ def tile_attend_twosources_distanceout_lean_pl_kernel(
         note_scales = tile([P, I], U8, "note_scales")
         nc.vector.quantize_mx(note_codes[:].bitcast(FP8X4), note_scales[:], notes_woven[:])
 
-        query_codes, query_scales = [], []
+        query_codes, query_scales = {}, {}
         for j in range(2):
             woven = tile([P, Q * PACK], BF16, f"query_woven{j}")
             nc.scalar.copy(
@@ -108,33 +109,26 @@ def tile_attend_twosources_distanceout_lean_pl_kernel(
             codes = tile([P, Q], U32, f"query_codes{j}")
             scales = tile([P, Q], U8, f"query_scales{j}")
             nc.vector.quantize_mx(codes[:].bitcast(FP8X4), scales[:], woven[:])
-            query_codes.append(codes)
-            query_scales.append(scales)
+            query_codes.setdefault(j, codes)
+            query_scales.setdefault(j, scales)
 
         weights_woven = tile([P, Q * PACK], BF16, "weights_woven")
         for h in range(Q // P):
             q_cols = slice(h * P, (h + 1) * P)
             scores = ps.tile([P, PACK, P], F32, name=f"scores{h}")
-            for t in range(PACK):
-                slots = slice(t * P, (t + 1) * P)
-                nc.tensor.matmul_mx(
-                    scores[:, t, :],
-                    lhsT=key_codes[:, slots].bitcast(FP4X4),
-                    lhsT_scale=key_code_scales[:, slots],
-                    rhs=query_codes[0][:, q_cols].bitcast(FP8X4),
-                    rhs_scale=query_scales[0][:, q_cols],
-                    start=True,
-                    stop=False,
-                )
-                nc.tensor.matmul_mx(
-                    scores[:, t, :],
-                    lhsT=note_codes[:, slots].bitcast(FP8X4),
-                    lhsT_scale=note_scales[:, slots],
-                    rhs=query_codes[1][:, q_cols].bitcast(FP8X4),
-                    rhs_scale=query_scales[1][:, q_cols],
-                    start=False,
-                    stop=True,
-                )
+            sources = ((key_codes, key_code_scales, FP4X4), (note_codes, note_scales, FP8X4))
+            for j, (codes, scales, packed_type) in enumerate(sources):
+                for t in range(PACK):
+                    slots = slice(t * P, (t + 1) * P)
+                    nc.tensor.matmul_mx(
+                        scores[:, t, :],
+                        lhsT=codes[:, slots].bitcast(packed_type),
+                        lhsT_scale=scales[:, slots],
+                        rhs=query_codes[j][:, q_cols].bitcast(FP8X4),
+                        rhs_scale=query_scales[j][:, q_cols],
+                        start=(j == 0 and t == 0),
+                        stop=(j == 1 and t == PACK - 1),
+                    )
             nc.vector.scalar_tensor_tensor(
                 weights_woven[:, h * P * PACK : (h + 1) * P * PACK].rearrange("p (q t) -> p q t", t=PACK),
                 scores[:].rearrange("p t q -> p q t"),
@@ -148,7 +142,6 @@ def tile_attend_twosources_distanceout_lean_pl_kernel(
         nc.vector.quantize_mx(weight_codes[:].bitcast(FP8X4), weight_scales[:], weights_woven[:])
 
         sums = []
-        dist = tile([P, PACK, Q], F32, "dist")
         halves = [slice(0, Q // 2), slice(Q // 2, Q)]
 
         def gather_values(r):
@@ -156,28 +149,30 @@ def tile_attend_twosources_distanceout_lean_pl_kernel(
             if r < PACK - 1:
                 nc.scalar.activation(listed_vals[:], val_planes[r][:].indirect(token_list[:]), ACT.Copy)
             else:
-                nc.vector.tensor_copy(listed_vals[:, : I // 2], val_planes[r][:].indirect(token_list[:, : I // 32]))
+                nc.vector.tensor_copy(listed_vals[:, :SPLIT], val_planes[r][:].indirect(token_list[:, : SPLIT // 16]))
                 nc.scalar.activation(
-                    listed_vals[:, I // 2 :], val_planes[r][:].indirect(token_list[:, I // 32 :]), ACT.Copy
+                    listed_vals[:, SPLIT:], val_planes[r][:].indirect(token_list[:, SPLIT // 16 :]), ACT.Copy
                 )
             return listed_vals
 
-        def multiply(r, listed_vals):
+        def quantise_values(r, listed_vals):
             pairs = listed_vals[:].bitcast(F32)
-            turned = ps_turn.tile([P, 2, P], F32, name="turned")
+            turned = ps.tile([P, 2, P], F32, name=f"turned{r}", tag="shared_bank" if r in (1, 2) else f"turned{r}")
             for u in range(2):
                 nc.tensor.transpose(turned[:, u, :], pairs[:, u::2], identity[:])
             vals_woven = tile([P, P * PACK], BF16, f"vals_woven{r}", tag="vals3" if r == PACK - 2 else None)
-            copy_out = nc.vector.tensor_copy if r < PACK - 1 else nc.scalar.copy
+            copy_out = nc.vector.tensor_copy if r < PACK - 2 else nc.scalar.copy
             copy_out(
                 vals_woven[:].bitcast(F32).rearrange("p (c u) -> p c u", u=2), turned[:].rearrange("p u c -> p c u")
             )
             val_codes = tile([P, P], U32, f"val_codes{r}")
             val_scales = tile([P, P], U8, f"val_scales{r}")
             nc.vector.quantize_mx(val_codes[:].bitcast(FP8X4), val_scales[:], vals_woven[:])
-            acc = ps.tile([P, Q], F32, name=f"acc{r}")
+            return val_codes, val_scales
+
+        def multiply(acc, val_codes, val_scales):
             nc.tensor.matmul_mx(
-                acc[:],
+                acc,
                 lhsT=val_codes[:].bitcast(FP8X4),
                 lhsT_scale=val_scales[:],
                 rhs=weight_codes[:].bitcast(FP8X4),
@@ -185,12 +180,8 @@ def tile_attend_twosources_distanceout_lean_pl_kernel(
                 start=True,
                 stop=True,
             )
-            o_plane = tile([P, Q], F32, f"o{r}")
-            copy_out = nc.vector.tensor_copy if r < PACK - 2 else nc.scalar.copy
-            copy_out(o_plane[:], acc[:])
-            sums.append(o_plane)
 
-        def distance(r):
+        def distance(r, dist):
             diff = tile([P, Q], F32, f"diff{r}")
             for cols in halves if r == PACK - 1 else [slice(0, Q)]:
                 listed = member_planes[r][:].indirect(member_list[:, cols.start // 16 : cols.stop // 16])
@@ -199,10 +190,23 @@ def tile_attend_twosources_distanceout_lean_pl_kernel(
             nc.sync.dma_start(planes_of(out_0)[:, r, :], dist[:, r, :])
 
         listed = [gather_values(r) for r in range(PACK)]
+        packed = [quantise_values(r, listed[r]) for r in range(2)]
+        early_acc = ps.tile([P, 2, Q], F32, name="early_acc", tag="shared_bank")
+        for r in range(2):
+            multiply(early_acc[:, r, :], *packed[r])
+        early_sums = tile([P, 2, Q], F32, "o_early")
+        nc.vector.tensor_copy(early_sums[:], early_acc[:])
+        sums.extend(early_sums[:, r, :] for r in range(2))
+        packed.extend(quantise_values(r, listed[r]) for r in range(2, PACK))
+        for r in range(2, PACK):
+            acc = ps.tile([P, Q], F32, name=f"acc{r}")
+            multiply(acc[:], *packed[r])
+            o_plane = tile([P, Q], F32, f"o{r}")
+            nc.scalar.copy(o_plane[:], acc[:])
+            sums.append(o_plane[:])
+        dist = tile([P, PACK, Q], F32, "dist")
         for r in range(PACK):
-            multiply(r, listed[r])
-        for r in range(PACK):
-            distance(r)
+            distance(r, dist)
         dist_woven = tile([P, Q * PACK], BF16, "dist_woven")
         dist_codes = tile([P, Q], U32, "dist_codes")
         dist_scales = tile([P, Q], U8, "dist_scales")

from contextlib import ExitStack

import concourse.mybir as mybir
from concourse.masks import make_identity

D, T, I, Q, E, U, M = 512, 2048, 512, 256, 512, 1024, 1024
FLOPS = 2 * Q * I * D * 2 + 2 * E * Q * I

F32 = mybir.dt.float32
BF16 = mybir.dt.bfloat16
I32 = mybir.dt.int32
U32 = mybir.dt.uint32
U16 = mybir.dt.uint16
U8 = mybir.dt.uint8
FP8X4 = mybir.dt.float8_e4m3fn_x4
FP4X4 = mybir.dt.float4_e2m1fn_x4
ALU = mybir.AluOpType
ACT = mybir.ActivationFunctionType

P = 128
PACK = 4
SPLIT = 288


def tile_attend_twosources_distanceout_lean_pl_kernel(
    tc, query, query2, keys_words, keys_scales, notes, slot_factor, vals, member, offs, offs2, offs3, out_0, out_1, out_2
):
    nc = tc.nc
    with ExitStack() as ctx:
        sb = ctx.enter_context(tc.tile_pool(name="sb", bufs=1))
        ps = ctx.enter_context(tc.psum_pool(name="ps", bufs=1))

        def tile(shape, dtype, name, tag=None):
            return sb.tile(shape, dtype, name=name, tag=tag or name, align_bytes=64)

        def planes_of(dram):
            return dram.rearrange("(p r) c -> p r c", r=PACK)

        token_list = tile([P, I // 16], U16, "token_list")
        note_list = tile([P, I // 16], U16, "note_list")
        member_list = tile([P, Q // 16], U16, "member_list")
        key_words = tile([P, T], U16, "key_words")
        key_scales = tile([P, T], U8, "key_scales")
        factor = tile([P, PACK], F32, "factor")
        note_planes = [tile([P, U], F32, f"notes{r}") for r in range(PACK)]
        val_planes = [tile([P, T], F32, f"vals{r}") for r in range(PACK)]
        member_planes = [tile([P, M], F32, f"member{r}") for r in range(PACK)]
        query_rows = [tile([P, PACK, Q], F32, f"query{j}") for j in range(2)]

        nc.vector.memset(key_scales[:].bitcast(I32), 0)
        for quad in range(4):
            nc.sync.dma_start(
                key_scales[32 * quad : 32 * quad + 4, :].bitcast(I32),
                keys_scales[0, 4 * quad : 4 * quad + 4, :].bitcast(I32),
            )
        nc.sync.dma_start(note_planes[0][:], planes_of(notes)[:, 0, :])
        nc.sync.dma_start(note_list[:], offs2)
        nc.sync.dma_start(key_words[:].bitcast(I32), keys_words[0].bitcast(I32))
        nc.sync.dma_start(token_list[:], offs)
        nc.sync.dma_start(query_rows[0][:], planes_of(query))
        for r in range(1, PACK):
            nc.sync.dma_start(note_planes[r][:], planes_of(notes)[:, r, :])
        nc.sync.dma_start(query_rows[1][:], planes_of(query2))
        nc.sync.dma_start(factor[:], slot_factor.rearrange("o (p t) -> (o p) t", t=PACK))
        nc.sync.dma_start(val_planes[0][:], planes_of(vals)[:, 0, :])
        nc.sync.dma_start(member_list[:], offs3)
        for r in range(1, PACK):
            nc.sync.dma_start(val_planes[r][:], planes_of(vals)[:, r, :])
        for r in range(PACK):
            nc.sync.dma_start(member_planes[r][:], planes_of(member)[:, r, :])

        identity = tile([P, P], F32, "identity")
        make_identity(nc, identity[:])

        listed_words = tile([P, I], U16, "listed_words")
        nc.vector.tensor_copy(listed_words[:], key_words[:].indirect(token_list[:]))
        key_codes = tile([P, I], U16, "key_codes")
        nc.vector.tensor_copy(
            key_codes[:].rearrange("p (t s) -> p s t", t=PACK), listed_words[:].rearrange("p (s t) -> p s t", t=PACK)
        )
        key_code_scales = tile([P, I], U8, "key_code_scales")
        nc.vector.tensor_copy(
            key_code_scales[:].rearrange("p (t s) -> p s t", t=PACK), key_scales[:].indirect(token_list[:])
        )

        listed_notes = tile([P, PACK, I], BF16, "listed_notes")
        for r in range(PACK):
            window = note_planes[r][:].indirect(note_list[:])
            if r < PACK - 1:
                nc.scalar.activation(listed_notes[:, r, :], window, ACT.Copy)
            else:
                nc.vector.tensor_copy(listed_notes[:, r, :], window)
        notes_woven = tile([P, I * PACK], BF16, "notes_woven")
        nc.vector.tensor_copy(
            notes_woven[:].rearrange("p (t s r) -> p s r t", t=PACK, r=PACK),
            listed_notes[:].rearrange("p r (s t) -> p s r t", t=PACK),
        )
        note_codes = tile([P, I], U32, "note_codes")
        note_scales = tile([P, I], U8, "note_scales")
        nc.vector.quantize_mx(note_codes[:].bitcast(FP8X4), note_scales[:], notes_woven[:])

        query_codes, query_scales = {}, {}
        for j in range(2):
            woven = tile([P, Q * PACK], BF16, f"query_woven{j}")
            nc.scalar.copy(
                woven[:].rearrange("p (c i r) -> p c r i", i=4, r=PACK),
                query_rows[j][:].rearrange("p r (c i) -> p c r i", i=4),
            )
            codes = tile([P, Q], U32, f"query_codes{j}")
            scales = tile([P, Q], U8, f"query_scales{j}")
            nc.vector.quantize_mx(codes[:].bitcast(FP8X4), scales[:], woven[:])
            query_codes.setdefault(j, codes)
            query_scales.setdefault(j, scales)

        weights_woven = tile([P, Q * PACK], BF16, "weights_woven")
        for h in range(Q // P):
            q_cols = slice(h * P, (h + 1) * P)
            scores = ps.tile([P, PACK, P], F32, name=f"scores{h}")
            sources = ((key_codes, key_code_scales, FP4X4), (note_codes, note_scales, FP8X4))
            for j, (codes, scales, packed_type) in enumerate(sources):
                for t in range(PACK):
                    slots = slice(t * P, (t + 1) * P)
                    nc.tensor.matmul_mx(
                        scores[:, t, :],
                        lhsT=codes[:, slots].bitcast(packed_type),
                        lhsT_scale=scales[:, slots],
                        rhs=query_codes[j][:, q_cols].bitcast(FP8X4),
                        rhs_scale=query_scales[j][:, q_cols],
                        start=(j == 0 and t == 0),
                        stop=(j == 1 and t == PACK - 1),
                    )
            nc.vector.scalar_tensor_tensor(
                weights_woven[:, h * P * PACK : (h + 1) * P * PACK].rearrange("p (q t) -> p q t", t=PACK),
                scores[:].rearrange("p t q -> p q t"),
                0.0,
                factor[:].unsqueeze(1).to_broadcast([P, P, PACK]),
                ALU.max,
                ALU.mult,
            )
        weight_codes = tile([P, Q], U32, "weight_codes")
        weight_scales = tile([P, Q], U8, "weight_scales")
        nc.vector.quantize_mx(weight_codes[:].bitcast(FP8X4), weight_scales[:], weights_woven[:])

        sums = []
        halves = [slice(0, Q // 2), slice(Q // 2, Q)]

        def gather_values(r):
            listed_vals = tile([P, I], BF16, f"listed_vals{r}")
            if r < PACK - 1:
                nc.scalar.activation(listed_vals[:], val_planes[r][:].indirect(token_list[:]), ACT.Copy)
            else:
                nc.vector.tensor_copy(listed_vals[:, :SPLIT], val_planes[r][:].indirect(token_list[:, : SPLIT // 16]))
                nc.scalar.activation(
                    listed_vals[:, SPLIT:], val_planes[r][:].indirect(token_list[:, SPLIT // 16 :]), ACT.Copy
                )
            return listed_vals

        def quantise_values(r, listed_vals):
            pairs = listed_vals[:].bitcast(F32)
            turned = ps.tile([P, 2, P], F32, name=f"turned{r}", tag="shared_bank" if r in (1, 2) else f"turned{r}")
            for u in range(2):
                nc.tensor.transpose(turned[:, u, :], pairs[:, u::2], identity[:])
            vals_woven = tile([P, P * PACK], BF16, f"vals_woven{r}", tag="vals3" if r == PACK - 2 else None)
            copy_out = nc.vector.tensor_copy if r < PACK - 2 else nc.scalar.copy
            copy_out(
                vals_woven[:].bitcast(F32).rearrange("p (c u) -> p c u", u=2), turned[:].rearrange("p u c -> p c u")
            )
            val_codes = tile([P, P], U32, f"val_codes{r}")
            val_scales = tile([P, P], U8, f"val_scales{r}")
            nc.vector.quantize_mx(val_codes[:].bitcast(FP8X4), val_scales[:], vals_woven[:])
            return val_codes, val_scales

        def multiply(acc, val_codes, val_scales):
            nc.tensor.matmul_mx(
                acc,
                lhsT=val_codes[:].bitcast(FP8X4),
                lhsT_scale=val_scales[:],
                rhs=weight_codes[:].bitcast(FP8X4),
                rhs_scale=weight_scales[:],
                start=True,
                stop=True,
            )

        def distance(r, dist):
            diff = tile([P, Q], F32, f"diff{r}")
            for cols in halves if r == PACK - 1 else [slice(0, Q)]:
                listed = member_planes[r][:].indirect(member_list[:, cols.start // 16 : cols.stop // 16])
                nc.vector.tensor_tensor(diff[:, cols], listed, sums[r][:, cols], ALU.subtract)
                nc.scalar.activation(dist[:, r, cols], diff[:, cols], ACT.Abs)
            nc.sync.dma_start(planes_of(out_0)[:, r, :], dist[:, r, :])

        listed = [gather_values(r) for r in range(PACK)]
        packed = [quantise_values(r, listed[r]) for r in range(2)]
        early_acc = ps.tile([P, 2, Q], F32, name="early_acc", tag="shared_bank")
        for r in range(2):
            multiply(early_acc[:, r, :], *packed[r])
        early_sums = tile([P, 2, Q], F32, "o_early")
        nc.vector.tensor_copy(early_sums[:], early_acc[:])
        sums.extend(early_sums[:, r, :] for r in range(2))
        packed.extend(quantise_values(r, listed[r]) for r in range(2, PACK))
        for r in range(2, PACK):
            acc = ps.tile([P, Q], F32, name=f"acc{r}")
            multiply(acc[:], *packed[r])
            o_plane = tile([P, Q], F32, f"o{r}")
            nc.scalar.copy(o_plane[:], acc[:])
            sums.append(o_plane[:])
        dist = tile([P, PACK, Q], F32, "dist")
        for r in range(PACK):
            distance(r, dist)
        dist_woven = tile([P, Q * PACK], BF16, "dist_woven")
        dist_codes = tile([P, Q], U32, "dist_codes")
        dist_scales = tile([P, Q], U8, "dist_scales")
        for cols in halves:
            nc.vector.tensor_copy(
                dist_woven[:, cols.start * PACK : cols.stop * PACK].rearrange("p (c i r) -> p c r i", i=4, r=PACK),
                dist[:, :, cols].rearrange("p r (c i) -> p c r i", i=4),
            )
        for cols in halves:
            nc.vector.quantize_mx(
                dist_codes[:, cols].bitcast(FP8X4),
                dist_scales[:, cols],
                dist_woven[:, cols.start * PACK : cols.stop * PACK],
            )
        nc.sync.dma_start(out_1[0].rearrange("p c r -> p (c r)").bitcast(I32), dist_codes[:].bitcast(I32))
        for quad in range(4):
            queue = nc.sync if quad % 2 == 0 else nc.scalar
            queue.dma_start(
                out_2[0, 4 * quad : 4 * quad + 4, :].bitcast(I32),
                dist_scales[32 * quad : 32 * quad + 4, :].bitcast(I32),
            )
